import numpy as np
import ml_dtypes


def mxq(x, axis, fmt="e4m3"):
    dtype, down = {"e4m3": (ml_dtypes.float8_e4m3fn, 7), "e5m2": (ml_dtypes.float8_e5m2, 14)}[fmt]
    v = np.moveaxis(np.asarray(x, np.float32).astype(ml_dtypes.bfloat16).astype(np.float64), axis, -1)
    blocks = v.reshape(v.shape[:-1] + (-1, 32))
    amax = np.abs(blocks).max(-1, keepdims=True)
    byte = np.maximum(np.where(amax > 0, np.frexp(amax)[1] - 1 + 127, 0) - down, 1)
    scale = np.exp2(byte - 127.0)
    codes = (blocks / scale).astype(np.float32).astype(dtype).astype(np.float64)
    return np.moveaxis((codes * scale).reshape(v.shape), -1, axis)


WIDE = False


def mx_kscale(k):
    if not WIDE:
        return np.ones(k)
    levels = np.array([10, -10, 5, -5, 0])
    if k % 512:
        return np.exp2(np.random.permutation(np.resize(levels, k // 32))).repeat(32)
    a = np.empty((k // 512, 16))
    for p in range(k // 512):
        a[p, :8] = np.random.permutation(np.resize(levels, 8))
        for g in range(8):
            far = levels[np.abs(levels - a[p, g]) >= 10]
            a[p, g + 8] = far[np.random.randint(len(far))]
    return np.exp2(a.ravel()).repeat(32)


def f64(x):
    return np.asarray(x).astype(np.float64)


def striped8(idx):
    return np.asarray(idx).reshape(8, -1, 16).transpose(0, 2, 1).reshape(128, -1).astype(np.uint16)


def unstriped8(offs):
    return offs.reshape(8, 16, -1).transpose(0, 2, 1).reshape(8, -1).astype(np.int64)


def pick8(x, idx, run):
    r = np.arange(len(x))
    return x[r[:, None], idx[r % (8 * run) // run]]


E2M1 = np.array([0.0, 0.5, 1.0, 1.5, 2.0, 3.0, 4.0, 6.0, -0.0, -0.5, -1.0, -1.5, -2.0, -3.0, -4.0, -6.0])


def pack_weight(w, fmt):
    k, n = w.shape
    w = f64(np.asarray(w, np.float32).astype(ml_dtypes.bfloat16)).reshape(k // 32, 32, n)
    amax = np.abs(w).max(1)
    if fmt == "e4m3":
        byte = np.frexp(amax)[1] - 1 + 127 - 7
    else:
        mant, ex = np.frexp(amax / 6.0)
        byte = np.where(mant > 0.5, ex, ex - 1) + 127
    byte = np.clip(np.where(amax > 0, byte, 1), 1, 254)
    scaled = (w * np.exp2(127.0 - byte)[:, None, :]).reshape(k, n).astype(np.float32)
    by_word = np.ascontiguousarray(scaled.reshape(k // 512, 128, 4, n).transpose(0, 1, 3, 2))
    if fmt == "e4m3":
        words = by_word.astype(ml_dtypes.float8_e4m3fn).view(np.uint8)
    else:
        c = by_word.astype(ml_dtypes.float4_e2m1fn).view(np.uint8) & 0xF
        words = (c[..., 0::2] | (c[..., 1::2] << 4)).reshape(k // 512, 128, 2 * n)
    return np.ascontiguousarray(words), np.ascontiguousarray(byte.astype(np.uint8).reshape(k // 512, 16, n))


def unpack_weight(words, scales, fmt):
    g, _, n = scales.shape
    words = np.ascontiguousarray(words).reshape(g, 128, n, -1)
    if fmt == "e4m3":
        vals = words.view(ml_dtypes.float8_e4m3fn).astype(np.float64)
    else:
        nib = np.empty((g, 128, n, 4), np.uint8)
        nib[..., 0::2] = words & 0xF
        nib[..., 1::2] = words >> 4
        vals = E2M1[nib]
    vals = vals * np.repeat(np.exp2(scales.astype(np.float64) - 127.0), 8, axis=1)[..., None]
    return vals.transpose(0, 1, 3, 2).reshape(g * 512, n)


D, K, T, I, Q = 512, 512, 1024, 512, 128


def setup_inputs():
    n = np.random.standard_normal
    idx = np.stack([np.random.permutation(T)[:I] for _ in range(8)])
    idx2 = np.stack([np.random.permutation(T)[:I] for _ in range(8)])
    idx3 = np.stack([np.random.permutation(T)[:I] for _ in range(8)])
    idx4 = np.stack([np.random.permutation(T)[:I] for _ in range(8)])
    fd = mx_kscale(D)
    fk = mx_kscale(K)
    wqp = pack_weight(n((D, K)) * 1.0 / np.sqrt(D) * fd[:, None] * fk, "e4m3")
    keysp = pack_weight(n((K, T)) * 1.0 / np.sqrt(K) / fk[:, None], "e2m1")
    tagsp = pack_weight(n((D, T)) * 0.5 / np.sqrt(D) * fd[:, None], "e4m3")
    return {
        "states": (n((D, Q)) * 0.95 / fd[:, None]).astype(np.float32),
        "wq_words": wqp[0],
        "wq_scales": wqp[1],
        "keys_words": keysp[0],
        "keys_scales": keysp[1],
        "tags_words": tagsp[0],
        "tags_scales": tagsp[1],
        "lam": (np.random.uniform(0.3, 0.8, (Q, 1))).astype(np.float32),
        "offs": striped8(idx),
        "offs2": striped8(idx2),
        "offs3": striped8(idx3),
        "offs4": striped8(idx4),
    }


def reference(states, wq_words, wq_scales, keys_words, keys_scales, tags_words, tags_scales, lam, offs, offs2, offs3, offs4):
    idx = unstriped8(offs)
    idx2 = unstriped8(offs2)
    idx3 = unstriped8(offs3)
    idx4 = unstriped8(offs4)
    wqu = unpack_weight(wq_words, wq_scales, "e4m3")
    keysu = unpack_weight(keys_words, keys_scales, "e2m1")
    tagsu = unpack_weight(tags_words, tags_scales, "e4m3")
    statesq = mxq(f64(states), 0, "e4m3")
    qv = wqu.T @ statesq
    qvq = mxq(qv, 0, "e4m3")
    a = qvq.T @ keysu + statesq.T @ tagsu
    r = pick8(a, idx2, 16) - pick8(a, idx, 16)
    f1 = np.zeros((Q, T))
    f1[np.arange(Q)[:, None], idx[np.arange(Q) % 128 // 16]] = r
    c1 = a + f1 * f64(lam)
    v = pick8(c1, idx3, 16) - pick8(c1, idx4, 16)
    f2 = np.zeros((Q, T))
    f2[np.arange(Q)[:, None], idx4[np.arange(Q) % 128 // 16]] = v
    c2 = c1 + f2 * f64(lam)
    y = pick8(c2, idx2, 16)
    return y

@@ -1,0 +1,174 @@
+from contextlib import ExitStack
+
+import concourse.mybir as mybir
+
+D, K, T, I, Q = 512, 512, 1024, 512, 128
+FLOPS = 2 * D * K * Q + 2 * K * T * Q + 2 * D * T * Q
+
+F32 = mybir.dt.float32
+BF16 = mybir.dt.bfloat16
+I32 = mybir.dt.int32
+U32 = mybir.dt.uint32
+U16 = mybir.dt.uint16
+U8 = mybir.dt.uint8
+FP8X4 = mybir.dt.float8_e4m3fn_x4
+FP4X4 = mybir.dt.float4_e2m1fn_x4
+MULT = mybir.AluOpType.mult
+ADD = mybir.AluOpType.add
+COPY = mybir.ActivationFunctionType.Copy
+
+P = 128
+PACK = 4
+N_BANK = 256
+HALF = I // 2
+HALF_COLS = HALF // 16
+Q_SPLIT = 96
+M_SPLIT = 80
+
+
+def load_scale_rows(nc, plane, scales, quads):
+    for quad in quads:
+        nc.sync.dma_start(
+            out=plane[32 * quad : 32 * quad + 4, :].bitcast(I32),
+            in_=scales[0, 4 * quad : 4 * quad + 4, :].bitcast(I32),
+        )
+
+
+def move_towards(nc, pool, name, cur, spread, lam_sb, to_list, from_list):
+    target = [pool.tile([P, HALF], F32, name=f"{name}_target{h}") for h in range(2)]
+    minus = [pool.tile([P, HALF], F32, name=f"{name}_minus{h}") for h in range(2)]
+    cols = [slice(h * HALF_COLS, (h + 1) * HALF_COLS) for h in range(2)]
+    nc.vector.tensor_scalar(minus[0][:], cur[:].indirect(from_list[:, cols[0]]), -1.0, 0.0, MULT, ADD)
+    nc.scalar.activation(target[0][:], cur[:].indirect(to_list[:, cols[0]]), COPY)
+    nc.scalar.activation(target[1][:], cur[:].indirect(to_list[:, cols[1]]), COPY)
+    nc.scalar.activation(minus[1][:], cur[:].indirect(from_list[:, cols[1]]), COPY, scale=-1.0)
+    for h in range(2):
+        nc.vector.tensor_tensor(spread[:].indirect(from_list[:, cols[h]]), target[h][:], minus[h][:], ADD)
+    nxt = pool.tile([P, T], F32, name=f"{name}_next")
+    nc.vector.scalar_tensor_tensor(nxt[:], spread[:], lam_sb[:], cur[:], MULT, ADD)
+    return nxt
+
+
+def tile_attend_settledtwice_madeparts_kernel(
+    tc, states, wq_words, wq_scales, keys_words, keys_scales, tags_words, tags_scales, lam, offs, offs2, offs3, offs4, out
+):
+    nc = tc.nc
+    with ExitStack() as ctx:
+        pool = ctx.enter_context(tc.tile_pool(name="held", bufs=1))
+        psum = ctx.enter_context(tc.psum_pool(name="psum", bufs=1))
+
+        st_raw = pool.tile([P, PACK, Q], F32, name="st_raw")
+        wq_raw = pool.tile([P, K], U32, name="wq_raw")
+        wq_sc_raw = pool.tile([P, K], U8, name="wq_sc_raw")
+        keys_sb = pool.tile([P, 2 * T], U8, name="keys_sb", align_bytes=64)
+        keys_sc = pool.tile([P, T], U8, name="keys_sc", align_bytes=64)
+        tags_sb = pool.tile([P, T], U32, name="tags_sb", align_bytes=64)
+        tags_sc = pool.tile([P, T], U8, name="tags_sc", align_bytes=64)
+        lam_sb = pool.tile([P, 1], F32, name="lam_sb")
+        lists = [pool.tile([P, I // 16], U16, name=f"list{n}") for n in range(4)]
+        f1 = pool.tile([P, T], F32, name="f1")
+        f2 = pool.tile([P, T], F32, name="f2")
+
+        nc.vector.memset(tags_sc[:].bitcast(I32), 0)
+        nc.vector.memset(keys_sc[:].bitcast(I32), 0)
+
+        nc.scalar.dma_start(out=st_raw[:], in_=states.rearrange("(p j) q -> p j q", j=PACK))
+        for quad in range(4):
+            rows = wq_scales[0, 4 * quad : 4 * quad + 4, :].bitcast(I32)
+            nc.sync.dma_start(
+                out=wq_sc_raw[32 * quad : 32 * quad + 32, :].bitcast(I32),
+                in_=rows.unsqueeze(0).to_broadcast([8, 4, K // 4]),
+            )
+        nc.sync.dma_start(out=wq_raw[:].bitcast(I32), in_=wq_words[0].rearrange("p c r -> p (c r)").bitcast(I32))
+        load_scale_rows(nc, tags_sc, tags_scales, (0, 1))
+        nc.sync.dma_start(out=tags_sb[:].bitcast(I32), in_=tags_words[0].rearrange("p c r -> p (c r)").bitcast(I32))
+        load_scale_rows(nc, tags_sc, tags_scales, (2, 3))
+        nc.sync.dma_start(out=keys_sb[:].bitcast(I32), in_=keys_words[0].bitcast(I32))
+        load_scale_rows(nc, keys_sc, keys_scales, (0, 1, 2, 3))
+        nc.sync.dma_start(lists[1][:], offs2)
+        nc.sync.dma_start(lists[0][:], offs)
+        nc.sync.dma_start(lists[2][:], offs3)
+        nc.sync.dma_start(lists[3][:], offs4)
+        nc.sync.dma_start(out=lam_sb[:], in_=lam)
+
+        nc.vector.memset(f1[:], 0.0)
+        nc.vector.memset(f2[:], 0.0)
+
+        wq_sc = pool.tile([P, PACK, P], U8, name="wq_sc", align_bytes=64)
+        nc.vector.tensor_copy(
+            out=wq_sc[:].rearrange("p t m -> p m t"), in_=wq_sc_raw[:].rearrange("p (m t) -> p m t", t=PACK)
+        )
+
+        st_bf = pool.tile([P, Q, PACK], BF16, name="st_bf", align_bytes=64)
+        st_dst = st_bf[:].rearrange("p (c i) t -> p c t i", i=4)
+        st_src = st_raw[:].rearrange("p t (c i) -> p c t i", i=4)
+        nc.vector.tensor_copy(out=st_dst[:, : Q_SPLIT // 4], in_=st_src[:, : Q_SPLIT // 4])
+        nc.scalar.activation(st_dst[:, Q_SPLIT // 4 :], st_src[:, Q_SPLIT // 4 :], COPY)
+        st_codes = pool.tile([P, Q], U32, name="st_codes", align_bytes=64)
+        st_sc = pool.tile([P, Q], U8, name="st_sc", align_bytes=64)
+        nc.vector.quantize_mx(out=st_codes[:].bitcast(FP8X4), scales=st_sc[:], in_=st_bf[:].rearrange("p q t -> p (q t)"))
+
+        wq_sb = pool.tile([P, PACK, P], U32, name="wq_sb", align_bytes=64)
+        wq_dst = wq_sb[:].rearrange("p t (b i) -> p b t i", i=4)
+        wq_src = wq_raw[:].rearrange("p (b i t) -> p b t i", i=4, t=PACK)
+        wq_dst_i = wq_sb[:].bitcast(I32).rearrange("p t (b i) -> p b t i", i=4)
+        wq_src_i = wq_raw[:].bitcast(I32).rearrange("p (b i t) -> p b t i", i=4, t=PACK)
+        nc.vector.tensor_copy(out=wq_dst_i[:, : M_SPLIT // 4], in_=wq_src_i[:, : M_SPLIT // 4])
+        nc.scalar.copy(out=wq_dst[:, M_SPLIT // 4 :], in_=wq_src[:, M_SPLIT // 4 :])
+
+        qv_ps = psum.tile([P, PACK, Q], F32, name="qv_ps")
+        for t in range(PACK):
+            nc.tensor.matmul_mx(
+                out=qv_ps[:, t, :],
+                lhsT=wq_sb[:, t, :].bitcast(FP8X4),
+                lhsT_scale=wq_sc[:, t, :],
+                rhs=st_codes[:].bitcast(FP8X4),
+                rhs_scale=st_sc[:],
+                start=True,
+                stop=True,
+            )
+
+        banks = [psum.tile([P, N_BANK], F32, name=f"bank{b}") for b in range(T // N_BANK)]
+        for b, bank in enumerate(banks):
+            cols = slice(b * N_BANK, (b + 1) * N_BANK)
+            nc.tensor.matmul_mx(
+                out=bank[:],
+                lhsT=st_codes[:].bitcast(FP8X4),
+                lhsT_scale=st_sc[:],
+                rhs=tags_sb[:, cols].bitcast(FP8X4),
+                rhs_scale=tags_sc[:, cols],
+                start=True,
+                stop=False,
+            )
+
+        qv_bf = pool.tile([P, Q, PACK], BF16, name="qv_bf", align_bytes=64)
+        nc.scalar.activation(qv_bf[:], qv_ps[:].rearrange("p t q -> p q t"), COPY)
+        qv_codes = pool.tile([P, Q], U32, name="qv_codes", align_bytes=64)
+        qv_sc = pool.tile([P, Q], U8, name="qv_sc", align_bytes=64)
+        nc.vector.quantize_mx(out=qv_codes[:].bitcast(FP8X4), scales=qv_sc[:], in_=qv_bf[:].rearrange("p q t -> p (q t)"))
+
+        a = pool.tile([P, T], F32, name="a")
+        for b, bank in enumerate(banks):
+            cols = slice(b * N_BANK, (b + 1) * N_BANK)
+            nc.tensor.matmul_mx(
+                out=bank[:],
+                lhsT=qv_codes[:].bitcast(FP8X4),
+                lhsT_scale=qv_sc[:],
+                rhs=keys_sb[:, 2 * b * N_BANK : 2 * (b + 1) * N_BANK].bitcast(FP4X4),
+                rhs_scale=keys_sc[:, cols],
+                start=False,
+                stop=True,
+            )
+            if b % 2 == 0:
+                nc.scalar.activation(a[:, cols], bank[:], COPY)
+            else:
+                nc.vector.tensor_copy(out=a[:, cols], in_=bank[:])
+
+        c1 = move_towards(nc, pool, "first", a, f1, lam_sb, lists[1], lists[0])
+        c2 = move_towards(nc, pool, "second", c1, f2, lam_sb, lists[2], lists[3])
+
+        y = [pool.tile([P, HALF], F32, name=f"y{h}") for h in range(2)]
+        nc.vector.tensor_copy(y[0][:], c2[:].indirect(lists[1][:, :HALF_COLS]))
+        nc.sync.dma_start(out=out[:, :HALF], in_=y[0][:])
+        nc.scalar.activation(y[1][:], c2[:].indirect(lists[1][:, HALF_COLS:]), COPY)
+        nc.scalar.dma_start(out=out[:, HALF:], in_=y[1][:])

@@ -19,11 +19,9 @@ COPY = mybir.ActivationFunctionType.Copy
 
 P = 128
 PACK = 4
-N_BANK = 256
+WIDTHS = (256, 256, 256, 128, 128)
 HALF = I // 2
 HALF_COLS = HALF // 16
-Q_SPLIT = 96
-M_SPLIT = 80
 
 
 def load_scale_rows(nc, plane, scales, quads):
@@ -72,17 +70,17 @@ def tile_attend_settledtwice_madeparts_kernel(
         nc.vector.memset(tags_sc[:].bitcast(I32), 0)
         nc.vector.memset(keys_sc[:].bitcast(I32), 0)
 
-        nc.scalar.dma_start(out=st_raw[:], in_=states.rearrange("(p j) q -> p j q", j=PACK))
-        for quad in range(4):
+        nc.sync.dma_start(out=st_raw[:], in_=states.rearrange("(p j) q -> p j q", j=PACK))
+        for quad, queue in enumerate((nc.scalar, nc.sync, nc.scalar, nc.sync)):
             rows = wq_scales[0, 4 * quad : 4 * quad + 4, :].bitcast(I32)
-            nc.sync.dma_start(
+            queue.dma_start(
                 out=wq_sc_raw[32 * quad : 32 * quad + 32, :].bitcast(I32),
                 in_=rows.unsqueeze(0).to_broadcast([8, 4, K // 4]),
             )
         nc.sync.dma_start(out=wq_raw[:].bitcast(I32), in_=wq_words[0].rearrange("p c r -> p (c r)").bitcast(I32))
-        load_scale_rows(nc, tags_sc, tags_scales, (0, 1))
+        load_scale_rows(nc, tags_sc, tags_scales, (0,))
         nc.sync.dma_start(out=tags_sb[:].bitcast(I32), in_=tags_words[0].rearrange("p c r -> p (c r)").bitcast(I32))
-        load_scale_rows(nc, tags_sc, tags_scales, (2, 3))
+        load_scale_rows(nc, tags_sc, tags_scales, (1, 2, 3))
         nc.sync.dma_start(out=keys_sb[:].bitcast(I32), in_=keys_words[0].bitcast(I32))
         load_scale_rows(nc, keys_sc, keys_scales, (0, 1, 2, 3))
         nc.sync.dma_start(lists[1][:], offs2)
@@ -96,25 +94,23 @@ def tile_attend_settledtwice_madeparts_kernel(
 
         wq_sc = pool.tile([P, PACK, P], U8, name="wq_sc", align_bytes=64)
         nc.vector.tensor_copy(
-            out=wq_sc[:].rearrange("p t m -> p m t"), in_=wq_sc_raw[:].rearrange("p (m t) -> p m t", t=PACK)
+            out=wq_sc[:].rearrange("p t (b i) -> p b t i", i=16),
+            in_=wq_sc_raw[:].rearrange("p (b i t) -> p b t i", i=16, t=PACK),
+        )
+
+        wq_sb = pool.tile([P, PACK, P], U32, name="wq_sb", align_bytes=64)
+        nc.vector.tensor_copy(
+            out=wq_sb[:].bitcast(I32).rearrange("p t (b i) -> p b t i", i=4),
+            in_=wq_raw[:].bitcast(I32).rearrange("p (b i t) -> p b t i", i=4, t=PACK),
         )
 
         st_bf = pool.tile([P, Q, PACK], BF16, name="st_bf", align_bytes=64)
         st_dst = st_bf[:].rearrange("p (c i) t -> p c t i", i=4)
         st_src = st_raw[:].rearrange("p t (c i) -> p c t i", i=4)
-        nc.vector.tensor_copy(out=st_dst[:, : Q_SPLIT // 4], in_=st_src[:, : Q_SPLIT // 4])
-        nc.scalar.activation(st_dst[:, Q_SPLIT // 4 :], st_src[:, Q_SPLIT // 4 :], COPY)
+        nc.scalar.activation(st_dst, st_src, COPY)
         st_codes = pool.tile([P, Q], U32, name="st_codes", align_bytes=64)
         st_sc = pool.tile([P, Q], U8, name="st_sc", align_bytes=64)
         nc.vector.quantize_mx(out=st_codes[:].bitcast(FP8X4), scales=st_sc[:], in_=st_bf[:].rearrange("p q t -> p (q t)"))
-
-        wq_sb = pool.tile([P, PACK, P], U32, name="wq_sb", align_bytes=64)
-        wq_dst = wq_sb[:].rearrange("p t (b i) -> p b t i", i=4)
-        wq_src = wq_raw[:].rearrange("p (b i t) -> p b t i", i=4, t=PACK)
-        wq_dst_i = wq_sb[:].bitcast(I32).rearrange("p t (b i) -> p b t i", i=4)
-        wq_src_i = wq_raw[:].bitcast(I32).rearrange("p (b i t) -> p b t i", i=4, t=PACK)
-        nc.vector.tensor_copy(out=wq_dst_i[:, : M_SPLIT // 4], in_=wq_src_i[:, : M_SPLIT // 4])
-        nc.scalar.copy(out=wq_dst[:, M_SPLIT // 4 :], in_=wq_src[:, M_SPLIT // 4 :])
 
         qv_ps = psum.tile([P, PACK, Q], F32, name="qv_ps")
         for t in range(PACK):
@@ -128,9 +124,9 @@ def tile_attend_settledtwice_madeparts_kernel(
                 stop=True,
             )
 
-        banks = [psum.tile([P, N_BANK], F32, name=f"bank{b}") for b in range(T // N_BANK)]
-        for b, bank in enumerate(banks):
-            cols = slice(b * N_BANK, (b + 1) * N_BANK)
+        banks = [psum.tile([P, w], F32, name=f"bank{b}") for b, w in enumerate(WIDTHS)]
+        spans = [slice(sum(WIDTHS[:b]), sum(WIDTHS[: b + 1])) for b in range(len(WIDTHS))]
+        for bank, cols in zip(banks, spans):
             nc.tensor.matmul_mx(
                 out=bank[:],
                 lhsT=st_codes[:].bitcast(FP8X4),
@@ -148,13 +144,12 @@ def tile_attend_settledtwice_madeparts_kernel(
         nc.vector.quantize_mx(out=qv_codes[:].bitcast(FP8X4), scales=qv_sc[:], in_=qv_bf[:].rearrange("p q t -> p (q t)"))
 
         a = pool.tile([P, T], F32, name="a")
-        for b, bank in enumerate(banks):
-            cols = slice(b * N_BANK, (b + 1) * N_BANK)
+        for b, (bank, cols) in enumerate(zip(banks, spans)):
             nc.tensor.matmul_mx(
                 out=bank[:],
                 lhsT=qv_codes[:].bitcast(FP8X4),
                 lhsT_scale=qv_sc[:],
-                rhs=keys_sb[:, 2 * b * N_BANK : 2 * (b + 1) * N_BANK].bitcast(FP4X4),
+                rhs=keys_sb[:, 2 * cols.start : 2 * cols.stop].bitcast(FP4X4),
                 rhs_scale=keys_sc[:, cols],
                 start=False,
                 stop=True,

from contextlib import ExitStack

import concourse.mybir as mybir

D, K, T, I, Q = 512, 512, 1024, 512, 128
FLOPS = 2 * D * K * Q + 2 * K * T * Q + 2 * D * T * Q

F32 = mybir.dt.float32
BF16 = mybir.dt.bfloat16
I32 = mybir.dt.int32
U32 = mybir.dt.uint32
U16 = mybir.dt.uint16
U8 = mybir.dt.uint8
FP8X4 = mybir.dt.float8_e4m3fn_x4
FP4X4 = mybir.dt.float4_e2m1fn_x4
MULT = mybir.AluOpType.mult
ADD = mybir.AluOpType.add
COPY = mybir.ActivationFunctionType.Copy

P = 128
PACK = 4
WIDTHS = (256, 256, 256, 128, 128)
HALF = I // 2
HALF_COLS = HALF // 16


def load_scale_rows(nc, plane, scales, quads):
    for quad in quads:
        nc.sync.dma_start(
            out=plane[32 * quad : 32 * quad + 4, :].bitcast(I32),
            in_=scales[0, 4 * quad : 4 * quad + 4, :].bitcast(I32),
        )


def move_towards(nc, pool, name, cur, spread, lam_sb, to_list, from_list):
    target = [pool.tile([P, HALF], F32, name=f"{name}_target{h}") for h in range(2)]
    minus = [pool.tile([P, HALF], F32, name=f"{name}_minus{h}") for h in range(2)]
    cols = [slice(h * HALF_COLS, (h + 1) * HALF_COLS) for h in range(2)]
    nc.vector.tensor_scalar(minus[0][:], cur[:].indirect(from_list[:, cols[0]]), -1.0, 0.0, MULT, ADD)
    nc.scalar.activation(target[0][:], cur[:].indirect(to_list[:, cols[0]]), COPY)
    nc.scalar.activation(target[1][:], cur[:].indirect(to_list[:, cols[1]]), COPY)
    nc.scalar.activation(minus[1][:], cur[:].indirect(from_list[:, cols[1]]), COPY, scale=-1.0)
    for h in range(2):
        nc.vector.tensor_tensor(spread[:].indirect(from_list[:, cols[h]]), target[h][:], minus[h][:], ADD)
    nxt = pool.tile([P, T], F32, name=f"{name}_next")
    nc.vector.scalar_tensor_tensor(nxt[:], spread[:], lam_sb[:], cur[:], MULT, ADD)
    return nxt


def tile_attend_settledtwice_madeparts_kernel(
    tc, states, wq_words, wq_scales, keys_words, keys_scales, tags_words, tags_scales, lam, offs, offs2, offs3, offs4, out
):
    nc = tc.nc
    with ExitStack() as ctx:
        pool = ctx.enter_context(tc.tile_pool(name="held", bufs=1))
        psum = ctx.enter_context(tc.psum_pool(name="psum", bufs=1))

        st_raw = pool.tile([P, PACK, Q], F32, name="st_raw")
        wq_raw = pool.tile([P, K], U32, name="wq_raw")
        wq_sc_raw = pool.tile([P, K], U8, name="wq_sc_raw")
        keys_sb = pool.tile([P, 2 * T], U8, name="keys_sb", align_bytes=64)
        keys_sc = pool.tile([P, T], U8, name="keys_sc", align_bytes=64)
        tags_sb = pool.tile([P, T], U32, name="tags_sb", align_bytes=64)
        tags_sc = pool.tile([P, T], U8, name="tags_sc", align_bytes=64)
        lam_sb = pool.tile([P, 1], F32, name="lam_sb")
        lists = [pool.tile([P, I // 16], U16, name=f"list{n}") for n in range(4)]
        f1 = pool.tile([P, T], F32, name="f1")
        f2 = pool.tile([P, T], F32, name="f2")

        nc.vector.memset(tags_sc[:].bitcast(I32), 0)
        nc.vector.memset(keys_sc[:].bitcast(I32), 0)

        nc.sync.dma_start(out=st_raw[:], in_=states.rearrange("(p j) q -> p j q", j=PACK))
        for quad, queue in enumerate((nc.scalar, nc.sync, nc.scalar, nc.sync)):
            rows = wq_scales[0, 4 * quad : 4 * quad + 4, :].bitcast(I32)
            queue.dma_start(
                out=wq_sc_raw[32 * quad : 32 * quad + 32, :].bitcast(I32),
                in_=rows.unsqueeze(0).to_broadcast([8, 4, K // 4]),
            )
        nc.sync.dma_start(out=wq_raw[:].bitcast(I32), in_=wq_words[0].rearrange("p c r -> p (c r)").bitcast(I32))
        load_scale_rows(nc, tags_sc, tags_scales, (0,))
        nc.sync.dma_start(out=tags_sb[:].bitcast(I32), in_=tags_words[0].rearrange("p c r -> p (c r)").bitcast(I32))
        load_scale_rows(nc, tags_sc, tags_scales, (1, 2, 3))
        nc.sync.dma_start(out=keys_sb[:].bitcast(I32), in_=keys_words[0].bitcast(I32))
        load_scale_rows(nc, keys_sc, keys_scales, (0, 1, 2, 3))
        nc.sync.dma_start(lists[1][:], offs2)
        nc.sync.dma_start(lists[0][:], offs)
        nc.sync.dma_start(lists[2][:], offs3)
        nc.sync.dma_start(lists[3][:], offs4)
        nc.sync.dma_start(out=lam_sb[:], in_=lam)

        nc.vector.memset(f1[:], 0.0)
        nc.vector.memset(f2[:], 0.0)

        wq_sc = pool.tile([P, PACK, P], U8, name="wq_sc", align_bytes=64)
        nc.vector.tensor_copy(
            out=wq_sc[:].rearrange("p t (b i) -> p b t i", i=16),
            in_=wq_sc_raw[:].rearrange("p (b i t) -> p b t i", i=16, t=PACK),
        )

        wq_sb = pool.tile([P, PACK, P], U32, name="wq_sb", align_bytes=64)
        nc.vector.tensor_copy(
            out=wq_sb[:].bitcast(I32).rearrange("p t (b i) -> p b t i", i=4),
            in_=wq_raw[:].bitcast(I32).rearrange("p (b i t) -> p b t i", i=4, t=PACK),
        )

        st_bf = pool.tile([P, Q, PACK], BF16, name="st_bf", align_bytes=64)
        st_dst = st_bf[:].rearrange("p (c i) t -> p c t i", i=4)
        st_src = st_raw[:].rearrange("p t (c i) -> p c t i", i=4)
        nc.scalar.activation(st_dst, st_src, COPY)
        st_codes = pool.tile([P, Q], U32, name="st_codes", align_bytes=64)
        st_sc = pool.tile([P, Q], U8, name="st_sc", align_bytes=64)
        nc.vector.quantize_mx(out=st_codes[:].bitcast(FP8X4), scales=st_sc[:], in_=st_bf[:].rearrange("p q t -> p (q t)"))

        qv_ps = psum.tile([P, PACK, Q], F32, name="qv_ps")
        for t in range(PACK):
            nc.tensor.matmul_mx(
                out=qv_ps[:, t, :],
                lhsT=wq_sb[:, t, :].bitcast(FP8X4),
                lhsT_scale=wq_sc[:, t, :],
                rhs=st_codes[:].bitcast(FP8X4),
                rhs_scale=st_sc[:],
                start=True,
                stop=True,
            )

        banks = [psum.tile([P, w], F32, name=f"bank{b}") for b, w in enumerate(WIDTHS)]
        spans = [slice(sum(WIDTHS[:b]), sum(WIDTHS[: b + 1])) for b in range(len(WIDTHS))]
        for bank, cols in zip(banks, spans):
            nc.tensor.matmul_mx(
                out=bank[:],
                lhsT=st_codes[:].bitcast(FP8X4),
                lhsT_scale=st_sc[:],
                rhs=tags_sb[:, cols].bitcast(FP8X4),
                rhs_scale=tags_sc[:, cols],
                start=True,
                stop=False,
            )

        qv_bf = pool.tile([P, Q, PACK], BF16, name="qv_bf", align_bytes=64)
        nc.scalar.activation(qv_bf[:], qv_ps[:].rearrange("p t q -> p q t"), COPY)
        qv_codes = pool.tile([P, Q], U32, name="qv_codes", align_bytes=64)
        qv_sc = pool.tile([P, Q], U8, name="qv_sc", align_bytes=64)
        nc.vector.quantize_mx(out=qv_codes[:].bitcast(FP8X4), scales=qv_sc[:], in_=qv_bf[:].rearrange("p q t -> p (q t)"))

        a = pool.tile([P, T], F32, name="a")
        for b, (bank, cols) in enumerate(zip(banks, spans)):
            nc.tensor.matmul_mx(
                out=bank[:],
                lhsT=qv_codes[:].bitcast(FP8X4),
                lhsT_scale=qv_sc[:],
                rhs=keys_sb[:, 2 * cols.start : 2 * cols.stop].bitcast(FP4X4),
                rhs_scale=keys_sc[:, cols],
                start=False,
                stop=True,
            )
            if b % 2 == 0:
                nc.scalar.activation(a[:, cols], bank[:], COPY)
            else:
                nc.vector.tensor_copy(out=a[:, cols], in_=bank[:])

        c1 = move_towards(nc, pool, "first", a, f1, lam_sb, lists[1], lists[0])
        c2 = move_towards(nc, pool, "second", c1, f2, lam_sb, lists[2], lists[3])

        y = [pool.tile([P, HALF], F32, name=f"y{h}") for h in range(2)]
        nc.vector.tensor_copy(y[0][:], c2[:].indirect(lists[1][:, :HALF_COLS]))
        nc.sync.dma_start(out=out[:, :HALF], in_=y[0][:])
        nc.scalar.activation(y[1][:], c2[:].indirect(lists[1][:, HALF_COLS:]), COPY)
        nc.scalar.dma_start(out=out[:, HALF:], in_=y[1][:])
